import numpy as np
import ml_dtypes


def mxq(x, axis, fmt="e4m3"):
    dtype, down = {"e4m3": (ml_dtypes.float8_e4m3fn, 7), "e5m2": (ml_dtypes.float8_e5m2, 14)}[fmt]
    v = np.moveaxis(np.asarray(x, np.float32).astype(ml_dtypes.bfloat16).astype(np.float64), axis, -1)
    blocks = v.reshape(v.shape[:-1] + (-1, 32))
    amax = np.abs(blocks).max(-1, keepdims=True)
    byte = np.maximum(np.where(amax > 0, np.frexp(amax)[1] - 1 + 127, 0) - down, 1)
    scale = np.exp2(byte - 127.0)
    codes = (blocks / scale).astype(np.float32).astype(dtype).astype(np.float64)
    return np.moveaxis((codes * scale).reshape(v.shape), -1, axis)


WIDE = False


def mx_kscale(k):
    if not WIDE:
        return np.ones(k)
    levels = np.array([10, -10, 5, -5, 0])
    if k % 512:
        return np.exp2(np.random.permutation(np.resize(levels, k // 32))).repeat(32)
    a = np.empty((k // 512, 16))
    for p in range(k // 512):
        a[p, :8] = np.random.permutation(np.resize(levels, 8))
        for g in range(8):
            far = levels[np.abs(levels - a[p, g]) >= 10]
            a[p, g + 8] = far[np.random.randint(len(far))]
    return np.exp2(a.ravel()).repeat(32)


def f64(x):
    return np.asarray(x).astype(np.float64)


def striped(idx):
    return np.tile(np.asarray(idx).reshape(-1, 16).T, (8, 1)).astype(np.uint16)


def unstriped(offs):
    return offs[:16].T.reshape(-1).astype(np.int64)


E2M1 = np.array([0.0, 0.5, 1.0, 1.5, 2.0, 3.0, 4.0, 6.0, -0.0, -0.5, -1.0, -1.5, -2.0, -3.0, -4.0, -6.0])


def pack_weight(w, fmt):
    k, n = w.shape
    w = f64(np.asarray(w, np.float32).astype(ml_dtypes.bfloat16)).reshape(k // 32, 32, n)
    amax = np.abs(w).max(1)
    if fmt == "e4m3":
        byte = np.frexp(amax)[1] - 1 + 127 - 7
    else:
        mant, ex = np.frexp(amax / 6.0)
        byte = np.where(mant > 0.5, ex, ex - 1) + 127
    byte = np.clip(np.where(amax > 0, byte, 1), 1, 254)
    scaled = (w * np.exp2(127.0 - byte)[:, None, :]).reshape(k, n).astype(np.float32)
    by_word = np.ascontiguousarray(scaled.reshape(k // 512, 128, 4, n).transpose(0, 1, 3, 2))
    if fmt == "e4m3":
        words = by_word.astype(ml_dtypes.float8_e4m3fn).view(np.uint8)
    else:
        c = by_word.astype(ml_dtypes.float4_e2m1fn).view(np.uint8) & 0xF
        words = (c[..., 0::2] | (c[..., 1::2] << 4)).reshape(k // 512, 128, 2 * n)
    return np.ascontiguousarray(words), np.ascontiguousarray(byte.astype(np.uint8).reshape(k // 512, 16, n))


def unpack_weight(words, scales, fmt):
    g, _, n = scales.shape
    words = np.ascontiguousarray(words).reshape(g, 128, n, -1)
    if fmt == "e4m3":
        vals = words.view(ml_dtypes.float8_e4m3fn).astype(np.float64)
    else:
        nib = np.empty((g, 128, n, 4), np.uint8)
        nib[..., 0::2] = words & 0xF
        nib[..., 1::2] = words >> 4
        vals = E2M1[nib]
    vals = vals * np.repeat(np.exp2(scales.astype(np.float64) - 127.0), 8, axis=1)[..., None]
    return vals.transpose(0, 1, 3, 2).reshape(g * 512, n)


D, E, T, I, Q, G = 512, 512, 2048, 512, 128, 64


def setup_inputs():
    n = np.random.standard_normal
    idx = np.random.permutation(T)[:I]
    fd = mx_kscale(D)
    fe = mx_kscale(E)
    keysp = pack_weight(n((D, T)) / fd[:, None], "e2m1")
    valsp = pack_weight(n((E, T)) / fe[:, None], "e2m1")
    return {
        "query": (n((D, Q)) * 0.8 / np.sqrt(D) * fd[:, None]).astype(np.float32),
        "query2": (n((D, Q)) * 0.8 / np.sqrt(D) * fd[:, None]).astype(np.float32),
        "keys_words": keysp[0],
        "keys_scales": keysp[1],
        "gout": (n((E, Q)) * 1 / np.sqrt(E) * fe[:, None]).astype(np.float32),
        "vals_words": valsp[0],
        "vals_scales": valsp[1],
        "base": (0.5 * n((Q, I))).astype(np.float32),
        "offs": striped(idx),
    }


def reference(query, query2, keys_words, keys_scales, gout, vals_words, vals_scales, base, offs):
    idx = unstriped(offs)
    keysu = unpack_weight(keys_words, keys_scales, "e2m1")
    valsu = unpack_weight(vals_words, vals_scales, "e2m1")
    queryq = mxq(f64(query), 0, "e4m3")
    keysidxg = keysu[:, idx]
    a = queryq.T @ keysidxg
    query2q = mxq(f64(query2), 0, "e4m3")
    b = query2q.T @ keysidxg
    pa = np.exp(a)
    sa = pa.reshape(Q, G, I // G).sum(axis=2)
    z = np.sum(sa, axis=1, keepdims=True)
    pb = np.exp(b)
    sb = pb.reshape(Q, G, I // G).sum(axis=2)
    goutq = mxq(f64(gout), 0, "e4m3")
    valsidxg = valsu[:, idx]
    c0 = goutq.T @ valsidxg
    drr = c0 * pb
    dr = drr.reshape(Q, G, I // G).sum(axis=2)
    dz = np.sum(dr / sb * sa / np.square(z) * (-1.0), axis=1, keepdims=True)
    dsa = dr / sb / z + dz
    r1 = np.repeat(dsa, I // G, axis=1)
    da = r1 * pa
    hda = da * 512.0 * 2.0 * 512.0
    hr1 = hda * pa
    hdsa = hr1.reshape(Q, G, I // G).sum(axis=2)
    hdz = np.sum(hdsa, axis=1, keepdims=True)
    hz = np.sum(hdsa * dr / sb / np.square(z) * (-1.0), axis=1, keepdims=True) + np.sum(hdz * (-1.0) * dr / sb * sa / np.square(np.square(z)) * (-1.0), axis=1, keepdims=True) * z * 2.0
    hsa = hdz * (-1.0) / np.square(z) * dr / sb + hz
    r51 = np.repeat(hsa, I // G, axis=1)
    hpa = hda * r1 + r51
    ha = hpa * pa
    y = ha + f64(base)
    return y

@@ -1,0 +1,250 @@
+import math
+from contextlib import ExitStack
+
+import concourse.mybir as mybir
+from concourse.masks import make_identity
+
+F32 = mybir.dt.float32
+BF16 = mybir.dt.bfloat16
+I32 = mybir.dt.int32
+U32 = mybir.dt.uint32
+U16 = mybir.dt.uint16
+U8 = mybir.dt.uint8
+FP8X4 = mybir.dt.float8_e4m3fn_x4
+FP4X4 = mybir.dt.float4_e2m1fn_x4
+ALU = mybir.AluOpType
+ACT = mybir.ActivationFunctionType
+AXIS_X = mybir.AxisListType.X
+
+P = 128
+PACK = 4
+POOL = 2048
+SLOTS = 512
+ROWS = 128
+PAGE = 8
+PAGES = SLOTS // PAGE
+HALF = SLOTS // 2
+
+ROOT_C = 512.0 * math.sqrt(2.0)
+SOFTEN = 4.0
+HEADROOM = 20.0
+
+FLOPS = 3 * 2 * 512 * ROWS * SLOTS
+
+
+def tile_attend_gppagethensecond_kernel(
+    tc, query, query2, keys_words, keys_scales, gout, vals_words, vals_scales, base, offs, out
+):
+    nc = tc.nc
+    with ExitStack() as ctx:
+        sb = ctx.enter_context(tc.tile_pool(name="sb", bufs=1))
+        ps = ctx.enter_context(tc.psum_pool(name="ps", bufs=1))
+
+        def tile(name, shape, dtype=F32, tag=None):
+            return sb.tile(shape, dtype, name=name, tag=tag or name, align_bytes=64)
+
+        def by_page(ap):
+            return ap.rearrange("p (g j) -> p g j", j=PAGE)
+
+        def over_page(ap):
+            return ap.unsqueeze(2).to_broadcast([P, ap.shape[1], PAGE])
+
+        offsets = tile("offsets", [P, SLOTS // 16], U16)
+        key_words = tile("key_words", [P, POOL], U16)
+        key_bytes = tile("key_bytes", [P, POOL], U8)
+        val_words = tile("val_words", [P, POOL], U16)
+        val_bytes = tile("val_bytes", [P, POOL], U8)
+        base_sb = tile("base_sb", [P, SLOTS])
+
+        nc.vector.memset(key_bytes[:].bitcast(I32), 0)
+        nc.gpsimd.memset(val_bytes[:].bitcast(I32), 0)
+        warm = tile("warm", [P, 1])
+        nc.vector.memset(warm[:], 0.0)
+        ident = tile("ident", [P, P])
+        make_identity(nc, ident[:])
+
+        def load_bytes(queue, dst, src):
+            for quad in range(4):
+                queue.dma_start(
+                    out=dst[32 * quad : 32 * quad + 4, :].bitcast(I32),
+                    in_=src[0, 4 * quad : 4 * quad + 4, :].bitcast(I32),
+                )
+
+        def load_rows(name, src):
+            raw = tile(name, [P, PACK, ROWS])
+            nc.sync.dma_start(out=raw[:], in_=src.rearrange("(p j) w -> p j w", j=PACK))
+            return raw
+
+        nc.sync.dma_start(offsets[:], offs)
+        nc.sync.dma_start(out=key_words[:].bitcast(I32), in_=keys_words[0].bitcast(I32))
+        load_bytes(nc.sync, key_bytes, keys_scales)
+        q1_raw = load_rows("q1_raw", query)
+        q2_raw = load_rows("q2_raw", query2)
+        go_raw = load_rows("go_raw", gout)
+        load_bytes(nc.sync, val_bytes, vals_scales)
+        nc.sync.dma_start(out=val_words[:].bitcast(I32), in_=vals_words[0].bitcast(I32))
+        nc.sync.dma_start(out=base_sb[:], in_=base)
+
+        warm_out = tile("warm_out", [P, 1])
+        nc.scalar.activation(warm_out[:], warm[:], ACT.Exp)
+
+        def interleave(name, raw):
+            grouped = tile(name, [P, ROWS, PACK], BF16)
+            nc.scalar.copy(out=grouped[:], in_=raw[:].rearrange("p j w -> p w j"))
+            return grouped
+
+        def quantize(name, grouped):
+            codes = tile(name + "_codes", [P, ROWS], U32)
+            scales = tile(name + "_scales", [P, ROWS], U8)
+            nc.vector.quantize_mx(
+                out=codes[:].bitcast(FP8X4), scales=scales[:], in_=grouped[:].rearrange("p w j -> p (w j)")
+            )
+            return codes, scales
+
+        def gather(name, window, dtype, tag=None):
+            picked = tile(name, [P, SLOTS], dtype, tag)
+            nc.vector.tensor_copy(picked[:], window[:].indirect(offsets[:]))
+            return picked
+
+        def product(name, rows, words, scale_bytes, bank):
+            acc = ps.tile([P, SLOTS], F32, name=name, tag=bank)
+            nc.tensor.matmul_mx(
+                out=acc[:],
+                lhsT=rows[0][:].bitcast(FP8X4),
+                lhsT_scale=rows[1][:],
+                rhs=words[:].bitcast(FP4X4),
+                rhs_scale=scale_bytes[:],
+                start=True,
+                stop=True,
+            )
+            return acc
+
+        q1_bf = interleave("q1_bf", q1_raw)
+        q2_bf = interleave("q2_bf", q2_raw)
+        go_bf = interleave("go_bf", go_raw)
+
+        kw = gather("kw", key_words, U16)
+        ks = gather("ks", key_bytes, U8)
+        q1_mx = quantize("q1", q1_bf)
+        q2_mx = quantize("q2", q2_bf)
+        a_ps = product("a_ps", q1_mx, kw, ks, "bank_a")
+        b_ps = product("b_ps", q2_mx, kw, ks, "bank_b")
+
+        pa = tile("pa", [P, SLOTS])
+        soft = tile("soft", [P, 1])
+        soft_terms = tile("soft_terms", [P, SLOTS], F32, "go_raw")
+        nc.scalar.activation(soft_terms[:], a_ps[:], ACT.Exp, scale=1.0 / SOFTEN, accum_out=soft[:])
+        shift = tile("shift", [P, 1])
+        nc.scalar.activation(
+            shift[:],
+            soft[:].bitcast(U32),
+            ACT.Copy,
+            scale=-SOFTEN * math.log(2.0) / 2.0**23,
+            bias=SOFTEN * math.log(2.0) * 127.0 + HEADROOM,
+        )
+        shift_two = tile("shift_two", [P, 1])
+        nc.scalar.activation(
+            shift_two[:],
+            soft[:].bitcast(U32),
+            ACT.Copy,
+            scale=-2.0 * SOFTEN * math.log(2.0) / 2.0**23,
+            bias=2.0 * (SOFTEN * math.log(2.0) * 127.0 + HEADROOM),
+        )
+        a_by_place = a_ps[:].rearrange("p (g j) -> p j g", j=PAGE)
+        slabs = [tile("slabs%d" % h, [P, PAGE // 2, 2, PAGES]) for h in range(2)]
+        for h in range(2):
+            places = a_by_place[:, 4 * h : 4 * h + 4, :]
+            nc.scalar.activation(slabs[h][:, :, 0, :], places, ACT.Exp, bias=shift[:])
+            nc.scalar.activation(slabs[h][:, :, 1, :], places, ACT.Exp, bias=shift_two[:], scale=2.0)
+
+        halves = [slice(0, HALF), slice(HALF, SLOTS)]
+        page_halves = [slice(0, PAGES // 2), slice(PAGES // 2, PAGES)]
+        vs = gather("vs", val_bytes, U8)
+        go_mx = quantize("go", go_bf)
+        top_b = [tile("top_b0", [P, PAGES // 2], F32, "val_bytes"), tile("top_b1", [P, PAGES // 2])]
+        db = [tile("db%d" % h, [P, HALF]) for h in range(2)]
+        pb = [tile("pb%d" % h, [P, HALF]) for h in range(2)]
+        for h in range(2):
+            nc.vector.tensor_reduce(top_b[h][:], by_page(b_ps[:, halves[h]]), AXIS_X, ALU.max)
+        for h in range(2):
+            nc.vector.tensor_tensor(by_page(db[h][:]), by_page(b_ps[:, halves[h]]), over_page(top_b[h][:]), ALU.subtract)
+        vw = gather("vw", val_words, U16, "val_bytes")
+
+        for h in range(2):
+            nc.scalar.activation(pb[h][:], db[h][:], ACT.Exp)
+        z = tile("z", [P, 1])
+        nc.scalar.activation(pa[:], a_ps[:], ACT.Exp, bias=shift[:], accum_out=z[:])
+
+        turned_ps = ps.tile([P, P], F32, name="turned_ps")
+        for j in range(PAGE):
+            nc.tensor.matmul(
+                turned_ps[:],
+                lhsT=slabs[j // 4][:, j % 4, :, :].rearrange("p k g -> p (k g)"),
+                rhs=ident[:],
+                is_transpose=True,
+                start=(j == 0),
+                stop=(j == PAGE - 1),
+            )
+        c_ps = product("c_ps", go_mx, vw, vs, "bank_c")
+        turned = tile("turned", [P, P])
+        nc.scalar.copy(turned[:], turned_ps[:])
+        sums_ps = ps.tile([P, P], F32, name="sums_ps")
+        nc.tensor.transpose(sums_ps[:], turned[:], ident[:])
+        sa = sums_ps[:, 0:PAGES]
+        sq_pa = sums_ps[:, PAGES : 2 * PAGES]
+
+        s_b = tile("s_b", [P, PAGES])
+        for h in range(2):
+            nc.vector.tensor_reduce(s_b[:, page_halves[h]], by_page(pb[h][:]), AXIS_X, ALU.add)
+        rz = tile("rz", [P, 1])
+        nc.vector.reciprocal(rz[:], z[:])
+
+        r_sq = tile("r_sq", [P, 1])
+        nc.scalar.activation(r_sq[:], rz[:], ACT.Square, scale=math.sqrt(ROOT_C / 2.0))
+        r_one = tile("r_one", [P, 1])
+        nc.scalar.activation(r_one[:], rz[:], ACT.Copy, scale=-ROOT_C)
+        r_two = tile("r_two", [P, 1])
+        nc.scalar.activation(r_two[:], rz[:], ACT.Copy, scale=-2.0 * ROOT_C)
+        q_one = tile("q_one", [P, PAGES])
+        nc.scalar.activation(q_one[:], sq_pa, ACT.Copy, scale=r_sq[:])
+        q_two = tile("q_two", [P, PAGES])
+        nc.scalar.activation(q_two[:], q_one[:], ACT.Copy, scale=r_two[:])
+
+        drr = tile("drr", [P, SLOTS])
+        for h in range(2):
+            nc.vector.tensor_tensor(drr[:, halves[h]], c_ps[:, halves[h]], pb[h][:], ALU.mult)
+        r_sb = tile("r_sb", [P, PAGES], F32, "pb0")
+        nc.vector.reciprocal(r_sb[:], s_b[:])
+        dr = tile("dr", [P, PAGES])
+        nc.vector.tensor_reduce(dr[:], by_page(drr[:]), AXIS_X, ALU.add)
+        weight = tile("weight", [P, PAGES])
+        nc.vector.tensor_tensor(weight[:], sa, r_sb[:], ALU.mult)
+        u = tile("u", [P, PAGES])
+        nc.vector.tensor_tensor(u[:], dr[:], r_sb[:], ALU.mult)
+        terms = tile("terms", [P, PAGES])
+        mean_u = tile("mean_u", [P, 1])
+        nc.vector.scalar_tensor_tensor(terms[:], dr[:], rz[:], weight[:], ALU.mult, ALU.mult, accum_out=mean_u[:])
+        vq_two = tile("vq_two", [P, PAGES])
+        nc.vector.scalar_tensor_tensor(vq_two[:], u[:], mean_u[:], q_two[:], ALU.subtract, ALU.mult)
+        vq_one = tile("vq_one", [P, PAGES])
+        beta = tile("beta", [P, 1])
+        nc.vector.scalar_tensor_tensor(vq_one[:], u[:], mean_u[:], q_one[:], ALU.subtract, ALU.mult, accum_out=beta[:])
+        kterms = tile("kterms", [P, PAGES])
+        kappa = tile("kappa", [P, 1])
+        nc.vector.scalar_tensor_tensor(kterms[:], u[:], mean_u[:], vq_two[:], ALU.subtract, ALU.mult, accum_out=kappa[:])
+        s = tile("s", [P, SLOTS])
+        nc.vector.scalar_tensor_tensor(
+            by_page(s[:]), over_page(u[:]), mean_u[:], by_page(pa[:]), ALU.subtract, ALU.mult
+        )
+
+        beta_sq = tile("beta_sq", [P, 1])
+        nc.scalar.activation(beta_sq[:], beta[:], ACT.Square)
+        square = [tile("square%d" % h, [P, HALF]) for h in range(2)]
+        for h in range(2):
+            nc.scalar.activation(square[h][:], s[:, halves[h]], ACT.Square, scale=r_one[:], bias=beta[:])
+        rest = tile("rest", [P, SLOTS])
+        nc.vector.scalar_tensor_tensor(rest[:], pa[:], kappa[:], base_sb[:], ALU.mult, ALU.add)
+        for h in range(2):
+            y = tile("y%d" % h, [P, HALF])
+            nc.vector.scalar_tensor_tensor(y[:], square[h][:], beta_sq[:], rest[:, halves[h]], ALU.subtract, ALU.add)
+            nc.sync.dma_start(out=out[:, halves[h]], in_=y[:])

@@ -64,11 +64,8 @@ def tile_attend_gppagethensecond_kernel(
         make_identity(nc, ident[:])
 
         def load_bytes(queue, dst, src):
-            for quad in range(4):
-                queue.dma_start(
-                    out=dst[32 * quad : 32 * quad + 4, :].bitcast(I32),
-                    in_=src[0, 4 * quad : 4 * quad + 4, :].bitcast(I32),
-                )
+            for row in range(4):
+                queue.dma_start(out=dst[row:P:32, :].bitcast(I32), in_=src[0, row:16:4, :].bitcast(I32))
 
         def load_rows(name, src):
             raw = tile(name, [P, PACK, ROWS])
@@ -90,7 +87,10 @@ def tile_attend_gppagethensecond_kernel(
 
         def interleave(name, raw):
             grouped = tile(name, [P, ROWS, PACK], BF16)
-            nc.scalar.copy(out=grouped[:], in_=raw[:].rearrange("p j w -> p w j"))
+            nc.scalar.copy(
+                out=grouped[:].rearrange("p (c i) j -> p c j i", i=4),
+                in_=raw[:].rearrange("p j (c i) -> p c j i", i=4),
+            )
             return grouped
 
         def quantize(name, grouped):
@@ -216,32 +216,43 @@ def tile_attend_gppagethensecond_kernel(
         r_sb = tile("r_sb", [P, PAGES], F32, "pb0")
         nc.vector.reciprocal(r_sb[:], s_b[:])
         dr = tile("dr", [P, PAGES])
-        nc.vector.tensor_reduce(dr[:], by_page(drr[:]), AXIS_X, ALU.add)
         weight = tile("weight", [P, PAGES])
+        nc.vector.tensor_reduce(dr[:, page_halves[0]], by_page(drr[:, halves[0]]), AXIS_X, ALU.add)
         nc.vector.tensor_tensor(weight[:], sa, r_sb[:], ALU.mult)
-        u = tile("u", [P, PAGES])
-        nc.vector.tensor_tensor(u[:], dr[:], r_sb[:], ALU.mult)
+        nc.vector.tensor_reduce(dr[:, page_halves[1]], by_page(drr[:, halves[1]]), AXIS_X, ALU.add)
         terms = tile("terms", [P, PAGES])
         mean_u = tile("mean_u", [P, 1])
         nc.vector.scalar_tensor_tensor(terms[:], dr[:], rz[:], weight[:], ALU.mult, ALU.mult, accum_out=mean_u[:])
+        u = tile("u", [P, PAGES])
+        nc.vector.tensor_tensor(u[:], dr[:], r_sb[:], ALU.mult)
         vq_two = tile("vq_two", [P, PAGES])
         nc.vector.scalar_tensor_tensor(vq_two[:], u[:], mean_u[:], q_two[:], ALU.subtract, ALU.mult)
         vq_one = tile("vq_one", [P, PAGES])
         beta = tile("beta", [P, 1])
         nc.vector.scalar_tensor_tensor(vq_one[:], u[:], mean_u[:], q_one[:], ALU.subtract, ALU.mult, accum_out=beta[:])
+        s = [tile("s%d" % h, [P, HALF]) for h in range(2)]
         kterms = tile("kterms", [P, PAGES])
         kappa = tile("kappa", [P, 1])
+
+        def centre(h):
+            nc.vector.scalar_tensor_tensor(
+                by_page(s[h][:]),
+                over_page(u[:, page_halves[h]]),
+                mean_u[:],
+                by_page(pa[:, halves[h]]),
+                ALU.subtract,
+                ALU.mult,
+            )
+
+        centre(0)
         nc.vector.scalar_tensor_tensor(kterms[:], u[:], mean_u[:], vq_two[:], ALU.subtract, ALU.mult, accum_out=kappa[:])
-        s = tile("s", [P, SLOTS])
-        nc.vector.scalar_tensor_tensor(
-            by_page(s[:]), over_page(u[:]), mean_u[:], by_page(pa[:]), ALU.subtract, ALU.mult
-        )
+        centre(1)
 
         beta_sq = tile("beta_sq", [P, 1])
         nc.scalar.activation(beta_sq[:], beta[:], ACT.Square)
         square = [tile("square%d" % h, [P, HALF]) for h in range(2)]
         for h in range(2):
-            nc.scalar.activation(square[h][:], s[:, halves[h]], ACT.Square, scale=r_one[:], bias=beta[:])
+            nc.scalar.activation(square[h][:], s[h][:], ACT.Square, scale=r_one[:], bias=beta[:])
         rest = tile("rest", [P, SLOTS])
         nc.vector.scalar_tensor_tensor(rest[:], pa[:], kappa[:], base_sb[:], ALU.mult, ALU.add)
         for h in range(2):

@@ -56,10 +56,10 @@ def tile_attend_gppagethensecond_kernel(
         val_bytes = tile("val_bytes", [P, POOL], U8)
         base_sb = tile("base_sb", [P, SLOTS])
 
-        nc.vector.memset(key_bytes[:].bitcast(I32), 0)
-        nc.gpsimd.memset(val_bytes[:].bitcast(I32), 0)
+        nc.gpsimd.memset(key_bytes[:].bitcast(I32), 0)
         warm = tile("warm", [P, 1])
         nc.vector.memset(warm[:], 0.0)
+        nc.vector.memset(val_bytes[:].bitcast(I32), 0)
         ident = tile("ident", [P, P])
         make_identity(nc, ident[:])
 
@@ -72,13 +72,13 @@ def tile_attend_gppagethensecond_kernel(
             nc.sync.dma_start(out=raw[:], in_=src.rearrange("(p j) w -> p j w", j=PACK))
             return raw
 
-        nc.sync.dma_start(offsets[:], offs)
         nc.sync.dma_start(out=key_words[:].bitcast(I32), in_=keys_words[0].bitcast(I32))
+        nc.sync.dma_start(offsets[:], offs)
         load_bytes(nc.sync, key_bytes, keys_scales)
         q1_raw = load_rows("q1_raw", query)
         q2_raw = load_rows("q2_raw", query2)
-        go_raw = load_rows("go_raw", gout)
         load_bytes(nc.sync, val_bytes, vals_scales)
+        go_raw = load_rows("go_raw", gout)
         nc.sync.dma_start(out=val_words[:].bitcast(I32), in_=vals_words[0].bitcast(I32))
         nc.sync.dma_start(out=base_sb[:], in_=base)
 
@@ -87,14 +87,11 @@ def tile_attend_gppagethensecond_kernel(
 
         def interleave(name, raw):
             grouped = tile(name, [P, ROWS, PACK], BF16)
-            nc.scalar.copy(
-                out=grouped[:].rearrange("p (c i) j -> p c j i", i=4),
-                in_=raw[:].rearrange("p j (c i) -> p c j i", i=4),
-            )
+            nc.scalar.copy(out=grouped[:], in_=raw[:].rearrange("p j w -> p w j"))
             return grouped
 
-        def quantize(name, grouped):
-            codes = tile(name + "_codes", [P, ROWS], U32)
+        def quantize(name, grouped, tag=None):
+            codes = tile(name + "_codes", [P, ROWS], U32, tag)
             scales = tile(name + "_scales", [P, ROWS], U8)
             nc.vector.quantize_mx(
                 out=codes[:].bitcast(FP8X4), scales=scales[:], in_=grouped[:].rearrange("p w j -> p (w j)")
@@ -121,7 +118,8 @@ def tile_attend_gppagethensecond_kernel(
 
         q1_bf = interleave("q1_bf", q1_raw)
         q2_bf = interleave("q2_bf", q2_raw)
-        go_bf = interleave("go_bf", go_raw)
+        go_bf = tile("go_bf", [P, ROWS, PACK], BF16)
+        nc.gpsimd.tensor_scalar(go_bf[:], go_raw[:].rearrange("p j w -> p w j"), 1.0, 0.0, ALU.mult, ALU.add)
 
         kw = gather("kw", key_words, U16)
         ks = gather("ks", key_bytes, U8)
@@ -130,9 +128,8 @@ def tile_attend_gppagethensecond_kernel(
         a_ps = product("a_ps", q1_mx, kw, ks, "bank_a")
         b_ps = product("b_ps", q2_mx, kw, ks, "bank_b")
 
-        pa = tile("pa", [P, SLOTS])
         soft = tile("soft", [P, 1])
-        soft_terms = tile("soft_terms", [P, SLOTS], F32, "go_raw")
+        soft_terms = tile("soft_terms", [P, SLOTS])
         nc.scalar.activation(soft_terms[:], a_ps[:], ACT.Exp, scale=1.0 / SOFTEN, accum_out=soft[:])
         shift = tile("shift", [P, 1])
         nc.scalar.activation(
@@ -152,15 +149,15 @@ def tile_attend_gppagethensecond_kernel(
         )
         a_by_place = a_ps[:].rearrange("p (g j) -> p j g", j=PAGE)
         slabs = [tile("slabs%d" % h, [P, PAGE // 2, 2, PAGES]) for h in range(2)]
+        z_half = [tile("z_half%d" % h, [P, 1]) for h in range(2)]
         for h in range(2):
             places = a_by_place[:, 4 * h : 4 * h + 4, :]
-            nc.scalar.activation(slabs[h][:, :, 0, :], places, ACT.Exp, bias=shift[:])
+            nc.scalar.activation(slabs[h][:, :, 0, :], places, ACT.Exp, bias=shift[:], accum_out=z_half[h][:])
             nc.scalar.activation(slabs[h][:, :, 1, :], places, ACT.Exp, bias=shift_two[:], scale=2.0)
 
         halves = [slice(0, HALF), slice(HALF, SLOTS)]
         page_halves = [slice(0, PAGES // 2), slice(PAGES // 2, PAGES)]
         vs = gather("vs", val_bytes, U8)
-        go_mx = quantize("go", go_bf)
         top_b = [tile("top_b0", [P, PAGES // 2], F32, "val_bytes"), tile("top_b1", [P, PAGES // 2])]
         db = [tile("db%d" % h, [P, HALF]) for h in range(2)]
         pb = [tile("pb%d" % h, [P, HALF]) for h in range(2)]
@@ -168,12 +165,18 @@ def tile_attend_gppagethensecond_kernel(
             nc.vector.tensor_reduce(top_b[h][:], by_page(b_ps[:, halves[h]]), AXIS_X, ALU.max)
         for h in range(2):
             nc.vector.tensor_tensor(by_page(db[h][:]), by_page(b_ps[:, halves[h]]), over_page(top_b[h][:]), ALU.subtract)
-        vw = gather("vw", val_words, U16, "val_bytes")
+        go_mx = quantize("go", go_bf, "val_bytes")
+        vw = gather("vw", val_words, U16, "top_b1")
 
         for h in range(2):
             nc.scalar.activation(pb[h][:], db[h][:], ACT.Exp)
         z = tile("z", [P, 1])
-        nc.scalar.activation(pa[:], a_ps[:], ACT.Exp, bias=shift[:], accum_out=z[:])
+        pa = tile("pa", [P, SLOTS], F32, "db0")
+        nc.scalar.activation(z[:], z_half[0][:], ACT.Identity, bias=z_half[1][:])
+        nc.scalar.activation(pa[:], a_ps[:], ACT.Exp, bias=shift[:])
+
+        rz = tile("rz", [P, 1], F32, "db1")
+        nc.vector.reciprocal(rz[:], z[:])
 
         turned_ps = ps.tile([P, P], F32, name="turned_ps")
         for j in range(PAGE):
@@ -186,7 +189,7 @@ def tile_attend_gppagethensecond_kernel(
                 stop=(j == PAGE - 1),
             )
         c_ps = product("c_ps", go_mx, vw, vs, "bank_c")
-        turned = tile("turned", [P, P])
+        turned = tile("turned", [P, P], F32, "shift")
         nc.scalar.copy(turned[:], turned_ps[:])
         sums_ps = ps.tile([P, P], F32, name="sums_ps")
         nc.tensor.transpose(sums_ps[:], turned[:], ident[:])
@@ -196,19 +199,15 @@ def tile_attend_gppagethensecond_kernel(
         s_b = tile("s_b", [P, PAGES])
         for h in range(2):
             nc.vector.tensor_reduce(s_b[:, page_halves[h]], by_page(pb[h][:]), AXIS_X, ALU.add)
-        rz = tile("rz", [P, 1])
-        nc.vector.reciprocal(rz[:], z[:])
 
         r_sq = tile("r_sq", [P, 1])
         nc.scalar.activation(r_sq[:], rz[:], ACT.Square, scale=math.sqrt(ROOT_C / 2.0))
-        r_one = tile("r_one", [P, 1])
-        nc.scalar.activation(r_one[:], rz[:], ACT.Copy, scale=-ROOT_C)
         r_two = tile("r_two", [P, 1])
-        nc.scalar.activation(r_two[:], rz[:], ACT.Copy, scale=-2.0 * ROOT_C)
+        nc.scalar.activation(r_two[:], rz[:], ACT.Copy, scale=2.0 * ROOT_C)
         q_one = tile("q_one", [P, PAGES])
         nc.scalar.activation(q_one[:], sq_pa, ACT.Copy, scale=r_sq[:])
-        q_two = tile("q_two", [P, PAGES])
-        nc.scalar.activation(q_two[:], q_one[:], ACT.Copy, scale=r_two[:])
+        pn = tile("pn", [P, SLOTS])
+        nc.scalar.activation(pn[:], pa[:], ACT.Copy, scale=r_two[:])
 
         drr = tile("drr", [P, SLOTS])
         for h in range(2):
@@ -225,8 +224,6 @@ def tile_attend_gppagethensecond_kernel(
         nc.vector.scalar_tensor_tensor(terms[:], dr[:], rz[:], weight[:], ALU.mult, ALU.mult, accum_out=mean_u[:])
         u = tile("u", [P, PAGES])
         nc.vector.tensor_tensor(u[:], dr[:], r_sb[:], ALU.mult)
-        vq_two = tile("vq_two", [P, PAGES])
-        nc.vector.scalar_tensor_tensor(vq_two[:], u[:], mean_u[:], q_two[:], ALU.subtract, ALU.mult)
         vq_one = tile("vq_one", [P, PAGES])
         beta = tile("beta", [P, 1])
         nc.vector.scalar_tensor_tensor(vq_one[:], u[:], mean_u[:], q_one[:], ALU.subtract, ALU.mult, accum_out=beta[:])
@@ -239,23 +236,23 @@ def tile_attend_gppagethensecond_kernel(
                 by_page(s[h][:]),
                 over_page(u[:, page_halves[h]]),
                 mean_u[:],
-                by_page(pa[:, halves[h]]),
+                by_page(pn[:, halves[h]]),
                 ALU.subtract,
                 ALU.mult,
             )
 
         centre(0)
-        nc.vector.scalar_tensor_tensor(kterms[:], u[:], mean_u[:], vq_two[:], ALU.subtract, ALU.mult, accum_out=kappa[:])
+        nc.vector.scalar_tensor_tensor(kterms[:], u[:], mean_u[:], vq_one[:], ALU.subtract, ALU.mult, accum_out=kappa[:])
         centre(1)
 
         beta_sq = tile("beta_sq", [P, 1])
         nc.scalar.activation(beta_sq[:], beta[:], ACT.Square)
         square = [tile("square%d" % h, [P, HALF]) for h in range(2)]
         for h in range(2):
-            nc.scalar.activation(square[h][:], s[h][:], ACT.Square, scale=r_one[:], bias=beta[:])
+            nc.scalar.activation(square[h][:], s[h][:], ACT.Square, scale=-0.5, bias=beta[:])
         rest = tile("rest", [P, SLOTS])
-        nc.vector.scalar_tensor_tensor(rest[:], pa[:], kappa[:], base_sb[:], ALU.mult, ALU.add)
+        nc.vector.scalar_tensor_tensor(rest[:], pn[:], kappa[:], base_sb[:], ALU.mult, ALU.subtract)
         for h in range(2):
             y = tile("y%d" % h, [P, HALF])
-            nc.vector.scalar_tensor_tensor(y[:], square[h][:], beta_sq[:], rest[:, halves[h]], ALU.subtract, ALU.add)
+            nc.vector.scalar_tensor_tensor(y[:], square[h][:], beta_sq[:], rest[:, halves[h]], ALU.subtract, ALU.subtract)
             nc.sync.dma_start(out=out[:, halves[h]], in_=y[:])

@@ -18,16 +18,22 @@ AXIS_X = mybir.AxisListType.X
 
 P = 128
 PACK = 4
+BLOCKS = 16
+QUADRANT = 32
 POOL = 2048
 SLOTS = 512
+LIST_ROWS = 16
 ROWS = 128
 PAGE = 8
 PAGES = SLOTS // PAGE
 HALF = SLOTS // 2
 
 ROOT_C = 512.0 * math.sqrt(2.0)
+
 SOFTEN = 4.0
 HEADROOM = 20.0
+LOG_SLOPE = SOFTEN * math.log(2.0) / 2.0**23
+LOG_OFFSET = SOFTEN * math.log(2.0) * 127.0 + HEADROOM
 
 FLOPS = 3 * 2 * 512 * ROWS * SLOTS
 
@@ -37,11 +43,11 @@ def tile_attend_gppagethensecond_kernel(
 ):
     nc = tc.nc
     with ExitStack() as ctx:
-        sb = ctx.enter_context(tc.tile_pool(name="sb", bufs=1))
-        ps = ctx.enter_context(tc.psum_pool(name="ps", bufs=1))
+        sbuf = ctx.enter_context(tc.tile_pool(name="sbuf", bufs=1))
+        psum = ctx.enter_context(tc.psum_pool(name="psum", bufs=1))
 
         def tile(name, shape, dtype=F32, tag=None):
-            return sb.tile(shape, dtype, name=name, tag=tag or name, align_bytes=64)
+            return sbuf.tile(shape, dtype, name=name, tag=tag or name, align_bytes=64)
 
         def by_page(ap):
             return ap.rearrange("p (g j) -> p g j", j=PAGE)
@@ -49,7 +55,10 @@ def tile_attend_gppagethensecond_kernel(
         def over_page(ap):
             return ap.unsqueeze(2).to_broadcast([P, ap.shape[1], PAGE])
 
-        offsets = tile("offsets", [P, SLOTS // 16], U16)
+        halves = [slice(0, HALF), slice(HALF, SLOTS)]
+        page_halves = [slice(0, PAGES // 2), slice(PAGES // 2, PAGES)]
+
+        offsets = tile("offsets", [P, SLOTS // LIST_ROWS], U16)
         key_words = tile("key_words", [P, POOL], U16)
         key_bytes = tile("key_bytes", [P, POOL], U8)
         val_words = tile("val_words", [P, POOL], U16)
@@ -57,15 +66,15 @@ def tile_attend_gppagethensecond_kernel(
         base_sb = tile("base_sb", [P, SLOTS])
 
         nc.gpsimd.memset(key_bytes[:].bitcast(I32), 0)
-        warm = tile("warm", [P, 1])
-        nc.vector.memset(warm[:], 0.0)
+        one = tile("one", [P, 1])
+        nc.vector.memset(one[:], 1.0)
         nc.vector.memset(val_bytes[:].bitcast(I32), 0)
         ident = tile("ident", [P, P])
         make_identity(nc, ident[:])
 
-        def load_bytes(queue, dst, src):
-            for row in range(4):
-                queue.dma_start(out=dst[row:P:32, :].bitcast(I32), in_=src[0, row:16:4, :].bitcast(I32))
+        def load_scale_rows(dst, src):
+            for r in range(4):
+                nc.sync.dma_start(out=dst[r:P:QUADRANT, :].bitcast(I32), in_=src[0, r:BLOCKS:4, :].bitcast(I32))
 
         def load_rows(name, src):
             raw = tile(name, [P, PACK, ROWS])
@@ -74,21 +83,26 @@ def tile_attend_gppagethensecond_kernel(
 
         nc.sync.dma_start(out=key_words[:].bitcast(I32), in_=keys_words[0].bitcast(I32))
         nc.sync.dma_start(offsets[:], offs)
-        load_bytes(nc.sync, key_bytes, keys_scales)
+        load_scale_rows(key_bytes, keys_scales)
         q1_raw = load_rows("q1_raw", query)
         q2_raw = load_rows("q2_raw", query2)
-        load_bytes(nc.sync, val_bytes, vals_scales)
+        load_scale_rows(val_bytes, vals_scales)
         go_raw = load_rows("go_raw", gout)
         nc.sync.dma_start(out=val_words[:].bitcast(I32), in_=vals_words[0].bitcast(I32))
         nc.sync.dma_start(out=base_sb[:], in_=base)
 
-        warm_out = tile("warm_out", [P, 1])
-        nc.scalar.activation(warm_out[:], warm[:], ACT.Exp)
+        log_offset = tile("log_offset", [P, 1])
+        nc.scalar.activation(log_offset[:], one[:], ACT.Exp, scale=math.log(LOG_OFFSET))
+        log_offset_two = tile("log_offset_two", [P, 1])
+        nc.scalar.activation(log_offset_two[:], log_offset[:], ACT.Copy, scale=2.0)
 
-        def interleave(name, raw):
-            grouped = tile(name, [P, ROWS, PACK], BF16)
-            nc.scalar.copy(out=grouped[:], in_=raw[:].rearrange("p j w -> p w j"))
-            return grouped
+        def round_on_scalar(grouped, raw, cols):
+            nc.scalar.copy(out=grouped[:, cols, :], in_=raw[:, :, cols].rearrange("p j w -> p w j"))
+
+        def round_on_gpsimd(grouped, raw, cols):
+            nc.gpsimd.tensor_scalar(
+                grouped[:, cols, :], raw[:, :, cols].rearrange("p j w -> p w j"), 1.0, 0.0, ALU.mult, ALU.add
+            )
 
         def quantize(name, grouped, tag=None):
             codes = tile(name + "_codes", [P, ROWS], U32, tag)
@@ -98,66 +112,61 @@ def tile_attend_gppagethensecond_kernel(
             )
             return codes, scales
 
-        def gather(name, window, dtype, tag=None):
-            picked = tile(name, [P, SLOTS], dtype, tag)
-            nc.vector.tensor_copy(picked[:], window[:].indirect(offsets[:]))
-            return picked
+        def gather(picked, window, slots):
+            listed = offsets[:, slots.start // LIST_ROWS : slots.stop // LIST_ROWS]
+            nc.vector.tensor_copy(picked[:, slots], window[:].indirect(listed))
 
-        def product(name, rows, words, scale_bytes, bank):
-            acc = ps.tile([P, SLOTS], F32, name=name, tag=bank)
+        def product(name, rows, words, scale_bytes, slots):
+            acc = psum.tile([P, slots.stop - slots.start], F32, name=name)
             nc.tensor.matmul_mx(
                 out=acc[:],
                 lhsT=rows[0][:].bitcast(FP8X4),
                 lhsT_scale=rows[1][:],
-                rhs=words[:].bitcast(FP4X4),
-                rhs_scale=scale_bytes[:],
+                rhs=words[:, slots].bitcast(FP4X4),
+                rhs_scale=scale_bytes[:, slots],
                 start=True,
                 stop=True,
             )
             return acc
 
-        q1_bf = interleave("q1_bf", q1_raw)
-        q2_bf = interleave("q2_bf", q2_raw)
+        q1_bf = tile("q1_bf", [P, ROWS, PACK], BF16)
+        q2_bf = tile("q2_bf", [P, ROWS, PACK], BF16)
         go_bf = tile("go_bf", [P, ROWS, PACK], BF16)
-        nc.gpsimd.tensor_scalar(go_bf[:], go_raw[:].rearrange("p j w -> p w j"), 1.0, 0.0, ALU.mult, ALU.add)
+        round_on_scalar(q1_bf, q1_raw, slice(0, ROWS))
+        round_on_scalar(q2_bf, q2_raw, slice(0, ROWS // 2))
+        round_on_gpsimd(q2_bf, q2_raw, slice(ROWS // 2, ROWS))
+        round_on_gpsimd(go_bf, go_raw, slice(0, ROWS))
 
-        kw = gather("kw", key_words, U16)
-        ks = gather("ks", key_bytes, U8)
+        all_slots = slice(0, SLOTS)
+        key_words_picked = tile("key_words_picked", [P, SLOTS], U16)
+        gather(key_words_picked, key_words, all_slots)
+        key_bytes_picked = tile("key_bytes_picked", [P, SLOTS], U8)
+        gather(key_bytes_picked, key_bytes, all_slots)
         q1_mx = quantize("q1", q1_bf)
         q2_mx = quantize("q2", q2_bf)
-        a_ps = product("a_ps", q1_mx, kw, ks, "bank_a")
-        b_ps = product("b_ps", q2_mx, kw, ks, "bank_b")
+        a_ps = product("a_ps", q1_mx, key_words_picked, key_bytes_picked, all_slots)
+        b_ps = product("b_ps", q2_mx, key_words_picked, key_bytes_picked, all_slots)
 
         soft = tile("soft", [P, 1])
         soft_terms = tile("soft_terms", [P, SLOTS])
         nc.scalar.activation(soft_terms[:], a_ps[:], ACT.Exp, scale=1.0 / SOFTEN, accum_out=soft[:])
-        shift = tile("shift", [P, 1])
+        minus_shift = tile("minus_shift", [P, 1])
+        nc.scalar.activation(minus_shift[:], soft[:].bitcast(U32), ACT.Identity, scale=-LOG_SLOPE, bias=log_offset[:])
+        minus_shift_two = tile("minus_shift_two", [P, 1])
         nc.scalar.activation(
-            shift[:],
-            soft[:].bitcast(U32),
-            ACT.Copy,
-            scale=-SOFTEN * math.log(2.0) / 2.0**23,
-            bias=SOFTEN * math.log(2.0) * 127.0 + HEADROOM,
+            minus_shift_two[:], soft[:].bitcast(U32), ACT.Identity, scale=-2.0 * LOG_SLOPE, bias=log_offset_two[:]
         )
-        shift_two = tile("shift_two", [P, 1])
-        nc.scalar.activation(
-            shift_two[:],
-            soft[:].bitcast(U32),
-            ACT.Copy,
-            scale=-2.0 * SOFTEN * math.log(2.0) / 2.0**23,
-            bias=2.0 * (SOFTEN * math.log(2.0) * 127.0 + HEADROOM),
-        )
+        places_a_half = PAGE // 2
         a_by_place = a_ps[:].rearrange("p (g j) -> p j g", j=PAGE)
-        slabs = [tile("slabs%d" % h, [P, PAGE // 2, 2, PAGES]) for h in range(2)]
+        slabs = [tile("slabs%d" % h, [P, places_a_half, 2, PAGES]) for h in range(2)]
         z_half = [tile("z_half%d" % h, [P, 1]) for h in range(2)]
         for h in range(2):
-            places = a_by_place[:, 4 * h : 4 * h + 4, :]
-            nc.scalar.activation(slabs[h][:, :, 0, :], places, ACT.Exp, bias=shift[:], accum_out=z_half[h][:])
-            nc.scalar.activation(slabs[h][:, :, 1, :], places, ACT.Exp, bias=shift_two[:], scale=2.0)
+            places = a_by_place[:, places_a_half * h : places_a_half * (h + 1), :]
+            nc.scalar.activation(slabs[h][:, :, 0, :], places, ACT.Exp, bias=minus_shift[:], accum_out=z_half[h][:])
+            nc.scalar.activation(slabs[h][:, :, 1, :], places, ACT.Exp, bias=minus_shift_two[:], scale=2.0)
 
-        halves = [slice(0, HALF), slice(HALF, SLOTS)]
-        page_halves = [slice(0, PAGES // 2), slice(PAGES // 2, PAGES)]
-        vs = gather("vs", val_bytes, U8)
+        val_bytes_picked = tile("val_bytes_picked", [P, SLOTS], U8)
+        gather(val_bytes_picked, val_bytes, all_slots)
         top_b = [tile("top_b0", [P, PAGES // 2], F32, "val_bytes"), tile("top_b1", [P, PAGES // 2])]
         db = [tile("db%d" % h, [P, HALF]) for h in range(2)]
         pb = [tile("pb%d" % h, [P, HALF]) for h in range(2)]
@@ -166,92 +175,88 @@ def tile_attend_gppagethensecond_kernel(
         for h in range(2):
             nc.vector.tensor_tensor(by_page(db[h][:]), by_page(b_ps[:, halves[h]]), over_page(top_b[h][:]), ALU.subtract)
         go_mx = quantize("go", go_bf, "val_bytes")
-        vw = gather("vw", val_words, U16, "top_b1")
+        val_words_picked = tile("val_words_picked", [P, SLOTS], U16, "top_b1")
+        for h in range(2):
+            gather(val_words_picked, val_words, halves[h])
 
         for h in range(2):
             nc.scalar.activation(pb[h][:], db[h][:], ACT.Exp)
         z = tile("z", [P, 1])
         pa = tile("pa", [P, SLOTS], F32, "db0")
         nc.scalar.activation(z[:], z_half[0][:], ACT.Identity, bias=z_half[1][:])
-        nc.scalar.activation(pa[:], a_ps[:], ACT.Exp, bias=shift[:])
+        nc.scalar.activation(pa[:], a_ps[:], ACT.Exp, bias=minus_shift[:])
+        r_z = tile("r_z", [P, 1], F32, "db1")
+        nc.vector.reciprocal(r_z[:], z[:])
 
-        rz = tile("rz", [P, 1], F32, "db1")
-        nc.vector.reciprocal(rz[:], z[:])
-
-        turned_ps = ps.tile([P, P], F32, name="turned_ps")
+        turned_ps = psum.tile([P, P], F32, name="turned_ps")
         for j in range(PAGE):
             nc.tensor.matmul(
                 turned_ps[:],
-                lhsT=slabs[j // 4][:, j % 4, :, :].rearrange("p k g -> p (k g)"),
+                lhsT=slabs[j // places_a_half][:, j % places_a_half, :, :].rearrange("p k g -> p (k g)"),
                 rhs=ident[:],
                 is_transpose=True,
                 start=(j == 0),
                 stop=(j == PAGE - 1),
             )
-        c_ps = product("c_ps", go_mx, vw, vs, "bank_c")
-        turned = tile("turned", [P, P], F32, "shift")
+        c_ps = [product("c_ps%d" % h, go_mx, val_words_picked, val_bytes_picked, halves[h]) for h in range(2)]
+        turned = tile("turned", [P, P], F32, "minus_shift")
         nc.scalar.copy(turned[:], turned_ps[:])
-        sums_ps = ps.tile([P, P], F32, name="sums_ps")
+        sums_ps = psum.tile([P, P], F32, name="sums_ps")
         nc.tensor.transpose(sums_ps[:], turned[:], ident[:])
-        sa = sums_ps[:, 0:PAGES]
-        sq_pa = sums_ps[:, PAGES : 2 * PAGES]
+        sum_pa = sums_ps[:, 0:PAGES]
+        sum_pa_sq = sums_ps[:, PAGES : 2 * PAGES]
 
-        s_b = tile("s_b", [P, PAGES])
+        sum_pb = tile("sum_pb", [P, PAGES])
         for h in range(2):
-            nc.vector.tensor_reduce(s_b[:, page_halves[h]], by_page(pb[h][:]), AXIS_X, ALU.add)
+            nc.vector.tensor_reduce(sum_pb[:, page_halves[h]], by_page(pb[h][:]), AXIS_X, ALU.add)
 
-        r_sq = tile("r_sq", [P, 1])
-        nc.scalar.activation(r_sq[:], rz[:], ACT.Square, scale=math.sqrt(ROOT_C / 2.0))
-        r_two = tile("r_two", [P, 1])
-        nc.scalar.activation(r_two[:], rz[:], ACT.Copy, scale=2.0 * ROOT_C)
-        q_one = tile("q_one", [P, PAGES])
-        nc.scalar.activation(q_one[:], sq_pa, ACT.Copy, scale=r_sq[:])
-        pn = tile("pn", [P, SLOTS])
-        nc.scalar.activation(pn[:], pa[:], ACT.Copy, scale=r_two[:])
+        q_factor = tile("q_factor", [P, 1])
+        nc.scalar.activation(q_factor[:], r_z[:], ACT.Square, scale=math.sqrt(ROOT_C / 2.0))
+        p_factor = tile("p_factor", [P, 1])
+        nc.scalar.activation(p_factor[:], r_z[:], ACT.Copy, scale=2.0 * ROOT_C)
+        q_scaled = tile("q_scaled", [P, PAGES])
+        nc.scalar.activation(q_scaled[:], sum_pa_sq, ACT.Copy, scale=q_factor[:])
+        p_scaled = tile("p_scaled", [P, SLOTS])
+        nc.scalar.activation(p_scaled[:], pa[:], ACT.Copy, scale=p_factor[:])
 
         drr = tile("drr", [P, SLOTS])
         for h in range(2):
-            nc.vector.tensor_tensor(drr[:, halves[h]], c_ps[:, halves[h]], pb[h][:], ALU.mult)
+            nc.vector.tensor_tensor(drr[:, halves[h]], c_ps[h][:], pb[h][:], ALU.mult)
         r_sb = tile("r_sb", [P, PAGES], F32, "pb0")
-        nc.vector.reciprocal(r_sb[:], s_b[:])
+        nc.vector.reciprocal(r_sb[:], sum_pb[:])
         dr = tile("dr", [P, PAGES])
-        weight = tile("weight", [P, PAGES])
+        sa_over_sb = tile("sa_over_sb", [P, PAGES])
         nc.vector.tensor_reduce(dr[:, page_halves[0]], by_page(drr[:, halves[0]]), AXIS_X, ALU.add)
-        nc.vector.tensor_tensor(weight[:], sa, r_sb[:], ALU.mult)
+        nc.vector.tensor_tensor(sa_over_sb[:], sum_pa, r_sb[:], ALU.mult)
         nc.vector.tensor_reduce(dr[:, page_halves[1]], by_page(drr[:, halves[1]]), AXIS_X, ALU.add)
-        terms = tile("terms", [P, PAGES])
+        mean_terms = tile("mean_terms", [P, PAGES])
         mean_u = tile("mean_u", [P, 1])
-        nc.vector.scalar_tensor_tensor(terms[:], dr[:], rz[:], weight[:], ALU.mult, ALU.mult, accum_out=mean_u[:])
+        nc.vector.scalar_tensor_tensor(
+            mean_terms[:], dr[:], r_z[:], sa_over_sb[:], ALU.mult, ALU.mult, accum_out=mean_u[:]
+        )
         u = tile("u", [P, PAGES])
         nc.vector.tensor_tensor(u[:], dr[:], r_sb[:], ALU.mult)
-        vq_one = tile("vq_one", [P, PAGES])
+
+        def times_v(dst, u_view, other, total=None):
+            nc.vector.scalar_tensor_tensor(dst, u_view, mean_u[:], other, ALU.subtract, ALU.mult, accum_out=total)
+
+        vq = tile("vq", [P, PAGES])
         beta = tile("beta", [P, 1])
-        nc.vector.scalar_tensor_tensor(vq_one[:], u[:], mean_u[:], q_one[:], ALU.subtract, ALU.mult, accum_out=beta[:])
-        s = [tile("s%d" % h, [P, HALF]) for h in range(2)]
-        kterms = tile("kterms", [P, PAGES])
+        times_v(vq[:], u[:], q_scaled[:], beta[:])
+        vp = [tile("vp%d" % h, [P, HALF]) for h in range(2)]
+        vvq = tile("vvq", [P, PAGES])
         kappa = tile("kappa", [P, 1])
-
-        def centre(h):
-            nc.vector.scalar_tensor_tensor(
-                by_page(s[h][:]),
-                over_page(u[:, page_halves[h]]),
-                mean_u[:],
-                by_page(pn[:, halves[h]]),
-                ALU.subtract,
-                ALU.mult,
-            )
-
-        centre(0)
-        nc.vector.scalar_tensor_tensor(kterms[:], u[:], mean_u[:], vq_one[:], ALU.subtract, ALU.mult, accum_out=kappa[:])
-        centre(1)
+        times_v(by_page(vp[0][:]), over_page(u[:, page_halves[0]]), by_page(p_scaled[:, halves[0]]))
+        times_v(vvq[:], u[:], vq[:], kappa[:])
+        times_v(by_page(vp[1][:]), over_page(u[:, page_halves[1]]), by_page(p_scaled[:, halves[1]]))
 
         beta_sq = tile("beta_sq", [P, 1])
         nc.scalar.activation(beta_sq[:], beta[:], ACT.Square)
         square = [tile("square%d" % h, [P, HALF]) for h in range(2)]
         for h in range(2):
-            nc.scalar.activation(square[h][:], s[h][:], ACT.Square, scale=-0.5, bias=beta[:])
+            nc.scalar.activation(square[h][:], vp[h][:], ACT.Square, scale=-0.5, bias=beta[:])
         rest = tile("rest", [P, SLOTS])
-        nc.vector.scalar_tensor_tensor(rest[:], pn[:], kappa[:], base_sb[:], ALU.mult, ALU.subtract)
+        nc.vector.scalar_tensor_tensor(rest[:], p_scaled[:], kappa[:], base_sb[:], ALU.mult, ALU.subtract)
         for h in range(2):
             y = tile("y%d" % h, [P, HALF])
             nc.vector.scalar_tensor_tensor(y[:], square[h][:], beta_sq[:], rest[:, halves[h]], ALU.subtract, ALU.subtract)

import math
from contextlib import ExitStack

import concourse.mybir as mybir
from concourse.masks import make_identity

F32 = mybir.dt.float32
BF16 = mybir.dt.bfloat16
I32 = mybir.dt.int32
U32 = mybir.dt.uint32
U16 = mybir.dt.uint16
U8 = mybir.dt.uint8
FP8X4 = mybir.dt.float8_e4m3fn_x4
FP4X4 = mybir.dt.float4_e2m1fn_x4
ALU = mybir.AluOpType
ACT = mybir.ActivationFunctionType
AXIS_X = mybir.AxisListType.X

P = 128
PACK = 4
BLOCKS = 16
QUADRANT = 32
POOL = 2048
SLOTS = 512
LIST_ROWS = 16
ROWS = 128
PAGE = 8
PAGES = SLOTS // PAGE
HALF = SLOTS // 2

ROOT_C = 512.0 * math.sqrt(2.0)

SOFTEN = 4.0
HEADROOM = 20.0
LOG_SLOPE = SOFTEN * math.log(2.0) / 2.0**23
LOG_OFFSET = SOFTEN * math.log(2.0) * 127.0 + HEADROOM

FLOPS = 3 * 2 * 512 * ROWS * SLOTS


def tile_attend_gppagethensecond_kernel(
    tc, query, query2, keys_words, keys_scales, gout, vals_words, vals_scales, base, offs, out
):
    nc = tc.nc
    with ExitStack() as ctx:
        sbuf = ctx.enter_context(tc.tile_pool(name="sbuf", bufs=1))
        psum = ctx.enter_context(tc.psum_pool(name="psum", bufs=1))

        def tile(name, shape, dtype=F32, tag=None):
            return sbuf.tile(shape, dtype, name=name, tag=tag or name, align_bytes=64)

        def by_page(ap):
            return ap.rearrange("p (g j) -> p g j", j=PAGE)

        def over_page(ap):
            return ap.unsqueeze(2).to_broadcast([P, ap.shape[1], PAGE])

        halves = [slice(0, HALF), slice(HALF, SLOTS)]
        page_halves = [slice(0, PAGES // 2), slice(PAGES // 2, PAGES)]

        offsets = tile("offsets", [P, SLOTS // LIST_ROWS], U16)
        key_words = tile("key_words", [P, POOL], U16)
        key_bytes = tile("key_bytes", [P, POOL], U8)
        val_words = tile("val_words", [P, POOL], U16)
        val_bytes = tile("val_bytes", [P, POOL], U8)
        base_sb = tile("base_sb", [P, SLOTS])

        nc.gpsimd.memset(key_bytes[:].bitcast(I32), 0)
        one = tile("one", [P, 1])
        nc.vector.memset(one[:], 1.0)
        nc.vector.memset(val_bytes[:].bitcast(I32), 0)
        ident = tile("ident", [P, P])
        make_identity(nc, ident[:])

        def load_scale_rows(dst, src):
            for r in range(4):
                nc.sync.dma_start(out=dst[r:P:QUADRANT, :].bitcast(I32), in_=src[0, r:BLOCKS:4, :].bitcast(I32))

        def load_rows(name, src):
            raw = tile(name, [P, PACK, ROWS])
            nc.sync.dma_start(out=raw[:], in_=src.rearrange("(p j) w -> p j w", j=PACK))
            return raw

        nc.sync.dma_start(out=key_words[:].bitcast(I32), in_=keys_words[0].bitcast(I32))
        nc.sync.dma_start(offsets[:], offs)
        load_scale_rows(key_bytes, keys_scales)
        q1_raw = load_rows("q1_raw", query)
        q2_raw = load_rows("q2_raw", query2)
        load_scale_rows(val_bytes, vals_scales)
        go_raw = load_rows("go_raw", gout)
        nc.sync.dma_start(out=val_words[:].bitcast(I32), in_=vals_words[0].bitcast(I32))
        nc.sync.dma_start(out=base_sb[:], in_=base)

        log_offset = tile("log_offset", [P, 1])
        nc.scalar.activation(log_offset[:], one[:], ACT.Exp, scale=math.log(LOG_OFFSET))
        log_offset_two = tile("log_offset_two", [P, 1])
        nc.scalar.activation(log_offset_two[:], log_offset[:], ACT.Copy, scale=2.0)

        def round_on_scalar(grouped, raw, cols):
            nc.scalar.copy(out=grouped[:, cols, :], in_=raw[:, :, cols].rearrange("p j w -> p w j"))

        def round_on_gpsimd(grouped, raw, cols):
            nc.gpsimd.tensor_scalar(
                grouped[:, cols, :], raw[:, :, cols].rearrange("p j w -> p w j"), 1.0, 0.0, ALU.mult, ALU.add
            )

        def quantize(name, grouped, tag=None):
            codes = tile(name + "_codes", [P, ROWS], U32, tag)
            scales = tile(name + "_scales", [P, ROWS], U8)
            nc.vector.quantize_mx(
                out=codes[:].bitcast(FP8X4), scales=scales[:], in_=grouped[:].rearrange("p w j -> p (w j)")
            )
            return codes, scales

        def gather(picked, window, slots):
            listed = offsets[:, slots.start // LIST_ROWS : slots.stop // LIST_ROWS]
            nc.vector.tensor_copy(picked[:, slots], window[:].indirect(listed))

        def product(name, rows, words, scale_bytes, slots):
            acc = psum.tile([P, slots.stop - slots.start], F32, name=name)
            nc.tensor.matmul_mx(
                out=acc[:],
                lhsT=rows[0][:].bitcast(FP8X4),
                lhsT_scale=rows[1][:],
                rhs=words[:, slots].bitcast(FP4X4),
                rhs_scale=scale_bytes[:, slots],
                start=True,
                stop=True,
            )
            return acc

        q1_bf = tile("q1_bf", [P, ROWS, PACK], BF16)
        q2_bf = tile("q2_bf", [P, ROWS, PACK], BF16)
        go_bf = tile("go_bf", [P, ROWS, PACK], BF16)
        round_on_scalar(q1_bf, q1_raw, slice(0, ROWS))
        round_on_scalar(q2_bf, q2_raw, slice(0, ROWS // 2))
        round_on_gpsimd(q2_bf, q2_raw, slice(ROWS // 2, ROWS))
        round_on_gpsimd(go_bf, go_raw, slice(0, ROWS))

        all_slots = slice(0, SLOTS)
        key_words_picked = tile("key_words_picked", [P, SLOTS], U16)
        gather(key_words_picked, key_words, all_slots)
        key_bytes_picked = tile("key_bytes_picked", [P, SLOTS], U8)
        gather(key_bytes_picked, key_bytes, all_slots)
        q1_mx = quantize("q1", q1_bf)
        q2_mx = quantize("q2", q2_bf)
        a_ps = product("a_ps", q1_mx, key_words_picked, key_bytes_picked, all_slots)
        b_ps = product("b_ps", q2_mx, key_words_picked, key_bytes_picked, all_slots)

        soft = tile("soft", [P, 1])
        soft_terms = tile("soft_terms", [P, SLOTS])
        nc.scalar.activation(soft_terms[:], a_ps[:], ACT.Exp, scale=1.0 / SOFTEN, accum_out=soft[:])
        minus_shift = tile("minus_shift", [P, 1])
        nc.scalar.activation(minus_shift[:], soft[:].bitcast(U32), ACT.Identity, scale=-LOG_SLOPE, bias=log_offset[:])
        minus_shift_two = tile("minus_shift_two", [P, 1])
        nc.scalar.activation(
            minus_shift_two[:], soft[:].bitcast(U32), ACT.Identity, scale=-2.0 * LOG_SLOPE, bias=log_offset_two[:]
        )
        places_a_half = PAGE // 2
        a_by_place = a_ps[:].rearrange("p (g j) -> p j g", j=PAGE)
        slabs = [tile("slabs%d" % h, [P, places_a_half, 2, PAGES]) for h in range(2)]
        z_half = [tile("z_half%d" % h, [P, 1]) for h in range(2)]
        for h in range(2):
            places = a_by_place[:, places_a_half * h : places_a_half * (h + 1), :]
            nc.scalar.activation(slabs[h][:, :, 0, :], places, ACT.Exp, bias=minus_shift[:], accum_out=z_half[h][:])
            nc.scalar.activation(slabs[h][:, :, 1, :], places, ACT.Exp, bias=minus_shift_two[:], scale=2.0)

        val_bytes_picked = tile("val_bytes_picked", [P, SLOTS], U8)
        gather(val_bytes_picked, val_bytes, all_slots)
        top_b = [tile("top_b0", [P, PAGES // 2], F32, "val_bytes"), tile("top_b1", [P, PAGES // 2])]
        db = [tile("db%d" % h, [P, HALF]) for h in range(2)]
        pb = [tile("pb%d" % h, [P, HALF]) for h in range(2)]
        for h in range(2):
            nc.vector.tensor_reduce(top_b[h][:], by_page(b_ps[:, halves[h]]), AXIS_X, ALU.max)
        for h in range(2):
            nc.vector.tensor_tensor(by_page(db[h][:]), by_page(b_ps[:, halves[h]]), over_page(top_b[h][:]), ALU.subtract)
        go_mx = quantize("go", go_bf, "val_bytes")
        val_words_picked = tile("val_words_picked", [P, SLOTS], U16, "top_b1")
        for h in range(2):
            gather(val_words_picked, val_words, halves[h])

        for h in range(2):
            nc.scalar.activation(pb[h][:], db[h][:], ACT.Exp)
        z = tile("z", [P, 1])
        pa = tile("pa", [P, SLOTS], F32, "db0")
        nc.scalar.activation(z[:], z_half[0][:], ACT.Identity, bias=z_half[1][:])
        nc.scalar.activation(pa[:], a_ps[:], ACT.Exp, bias=minus_shift[:])
        r_z = tile("r_z", [P, 1], F32, "db1")
        nc.vector.reciprocal(r_z[:], z[:])

        turned_ps = psum.tile([P, P], F32, name="turned_ps")
        for j in range(PAGE):
            nc.tensor.matmul(
                turned_ps[:],
                lhsT=slabs[j // places_a_half][:, j % places_a_half, :, :].rearrange("p k g -> p (k g)"),
                rhs=ident[:],
                is_transpose=True,
                start=(j == 0),
                stop=(j == PAGE - 1),
            )
        c_ps = [product("c_ps%d" % h, go_mx, val_words_picked, val_bytes_picked, halves[h]) for h in range(2)]
        turned = tile("turned", [P, P], F32, "minus_shift")
        nc.scalar.copy(turned[:], turned_ps[:])
        sums_ps = psum.tile([P, P], F32, name="sums_ps")
        nc.tensor.transpose(sums_ps[:], turned[:], ident[:])
        sum_pa = sums_ps[:, 0:PAGES]
        sum_pa_sq = sums_ps[:, PAGES : 2 * PAGES]

        sum_pb = tile("sum_pb", [P, PAGES])
        for h in range(2):
            nc.vector.tensor_reduce(sum_pb[:, page_halves[h]], by_page(pb[h][:]), AXIS_X, ALU.add)

        q_factor = tile("q_factor", [P, 1])
        nc.scalar.activation(q_factor[:], r_z[:], ACT.Square, scale=math.sqrt(ROOT_C / 2.0))
        p_factor = tile("p_factor", [P, 1])
        nc.scalar.activation(p_factor[:], r_z[:], ACT.Copy, scale=2.0 * ROOT_C)
        q_scaled = tile("q_scaled", [P, PAGES])
        nc.scalar.activation(q_scaled[:], sum_pa_sq, ACT.Copy, scale=q_factor[:])
        p_scaled = tile("p_scaled", [P, SLOTS])
        nc.scalar.activation(p_scaled[:], pa[:], ACT.Copy, scale=p_factor[:])

        drr = tile("drr", [P, SLOTS])
        for h in range(2):
            nc.vector.tensor_tensor(drr[:, halves[h]], c_ps[h][:], pb[h][:], ALU.mult)
        r_sb = tile("r_sb", [P, PAGES], F32, "pb0")
        nc.vector.reciprocal(r_sb[:], sum_pb[:])
        dr = tile("dr", [P, PAGES])
        sa_over_sb = tile("sa_over_sb", [P, PAGES])
        nc.vector.tensor_reduce(dr[:, page_halves[0]], by_page(drr[:, halves[0]]), AXIS_X, ALU.add)
        nc.vector.tensor_tensor(sa_over_sb[:], sum_pa, r_sb[:], ALU.mult)
        nc.vector.tensor_reduce(dr[:, page_halves[1]], by_page(drr[:, halves[1]]), AXIS_X, ALU.add)
        mean_terms = tile("mean_terms", [P, PAGES])
        mean_u = tile("mean_u", [P, 1])
        nc.vector.scalar_tensor_tensor(
            mean_terms[:], dr[:], r_z[:], sa_over_sb[:], ALU.mult, ALU.mult, accum_out=mean_u[:]
        )
        u = tile("u", [P, PAGES])
        nc.vector.tensor_tensor(u[:], dr[:], r_sb[:], ALU.mult)

        def times_v(dst, u_view, other, total=None):
            nc.vector.scalar_tensor_tensor(dst, u_view, mean_u[:], other, ALU.subtract, ALU.mult, accum_out=total)

        vq = tile("vq", [P, PAGES])
        beta = tile("beta", [P, 1])
        times_v(vq[:], u[:], q_scaled[:], beta[:])
        vp = [tile("vp%d" % h, [P, HALF]) for h in range(2)]
        vvq = tile("vvq", [P, PAGES])
        kappa = tile("kappa", [P, 1])
        times_v(by_page(vp[0][:]), over_page(u[:, page_halves[0]]), by_page(p_scaled[:, halves[0]]))
        times_v(vvq[:], u[:], vq[:], kappa[:])
        times_v(by_page(vp[1][:]), over_page(u[:, page_halves[1]]), by_page(p_scaled[:, halves[1]]))

        beta_sq = tile("beta_sq", [P, 1])
        nc.scalar.activation(beta_sq[:], beta[:], ACT.Square)
        square = [tile("square%d" % h, [P, HALF]) for h in range(2)]
        for h in range(2):
            nc.scalar.activation(square[h][:], vp[h][:], ACT.Square, scale=-0.5, bias=beta[:])
        rest = tile("rest", [P, SLOTS])
        nc.vector.scalar_tensor_tensor(rest[:], p_scaled[:], kappa[:], base_sb[:], ALU.mult, ALU.subtract)
        for h in range(2):
            y = tile("y%d" % h, [P, HALF])
            nc.vector.scalar_tensor_tensor(y[:], square[h][:], beta_sq[:], rest[:, halves[h]], ALU.subtract, ALU.subtract)
            nc.sync.dma_start(out=out[:, halves[h]], in_=y[:])
